import numpy as np
import ml_dtypes


def mxq(x, axis, fmt="e4m3"):
    dtype, down = {"e4m3": (ml_dtypes.float8_e4m3fn, 7), "e5m2": (ml_dtypes.float8_e5m2, 14)}[fmt]
    v = np.moveaxis(np.asarray(x, np.float32).astype(ml_dtypes.bfloat16).astype(np.float64), axis, -1)
    blocks = v.reshape(v.shape[:-1] + (-1, 32))
    amax = np.abs(blocks).max(-1, keepdims=True)
    byte = np.maximum(np.where(amax > 0, np.frexp(amax)[1] - 1 + 127, 0) - down, 1)
    scale = np.exp2(byte - 127.0)
    codes = (blocks / scale).astype(np.float32).astype(dtype).astype(np.float64)
    return np.moveaxis((codes * scale).reshape(v.shape), -1, axis)


WIDE = False


def mx_kscale(k):
    if not WIDE:
        return np.ones(k)
    levels = np.array([10, -10, 5, -5, 0])
    if k % 512:
        return np.exp2(np.random.permutation(np.resize(levels, k // 32))).repeat(32)
    a = np.empty((k // 512, 16))
    for p in range(k // 512):
        a[p, :8] = np.random.permutation(np.resize(levels, 8))
        for g in range(8):
            far = levels[np.abs(levels - a[p, g]) >= 10]
            a[p, g + 8] = far[np.random.randint(len(far))]
    return np.exp2(a.ravel()).repeat(32)


def f64(x):
    return np.asarray(x).astype(np.float64)


def striped8(idx):
    return np.asarray(idx).reshape(8, -1, 16).transpose(0, 2, 1).reshape(128, -1).astype(np.uint16)


def unstriped8(offs):
    return offs.reshape(8, 16, -1).transpose(0, 2, 1).reshape(8, -1).astype(np.int64)


def pick8(x, idx, run):
    r = np.arange(len(x))
    return x[r[:, None], idx[r % (8 * run) // run]]


E2M1 = np.array([0.0, 0.5, 1.0, 1.5, 2.0, 3.0, 4.0, 6.0, -0.0, -0.5, -1.0, -1.5, -2.0, -3.0, -4.0, -6.0])


def pack_weight(w, fmt):
    k, n = w.shape
    w = f64(np.asarray(w, np.float32).astype(ml_dtypes.bfloat16)).reshape(k // 32, 32, n)
    amax = np.abs(w).max(1)
    if fmt == "e4m3":
        byte = np.frexp(amax)[1] - 1 + 127 - 7
    else:
        mant, ex = np.frexp(amax / 6.0)
        byte = np.where(mant > 0.5, ex, ex - 1) + 127
    byte = np.clip(np.where(amax > 0, byte, 1), 1, 254)
    scaled = (w * np.exp2(127.0 - byte)[:, None, :]).reshape(k, n).astype(np.float32)
    by_word = np.ascontiguousarray(scaled.reshape(k // 512, 128, 4, n).transpose(0, 1, 3, 2))
    if fmt == "e4m3":
        words = by_word.astype(ml_dtypes.float8_e4m3fn).view(np.uint8)
    else:
        c = by_word.astype(ml_dtypes.float4_e2m1fn).view(np.uint8) & 0xF
        words = (c[..., 0::2] | (c[..., 1::2] << 4)).reshape(k // 512, 128, 2 * n)
    return np.ascontiguousarray(words), np.ascontiguousarray(byte.astype(np.uint8).reshape(k // 512, 16, n))


def unpack_weight(words, scales, fmt):
    g, _, n = scales.shape
    words = np.ascontiguousarray(words).reshape(g, 128, n, -1)
    if fmt == "e4m3":
        vals = words.view(ml_dtypes.float8_e4m3fn).astype(np.float64)
    else:
        nib = np.empty((g, 128, n, 4), np.uint8)
        nib[..., 0::2] = words & 0xF
        nib[..., 1::2] = words >> 4
        vals = E2M1[nib]
    vals = vals * np.repeat(np.exp2(scales.astype(np.float64) - 127.0), 8, axis=1)[..., None]
    return vals.transpose(0, 1, 3, 2).reshape(g * 512, n)


def sigmoid(v):
    return 1.0 / (1.0 + np.exp(-v))


D, K, T, I, Q = 512, 512, 1024, 512, 128


def setup_inputs():
    n = np.random.standard_normal
    idx = np.stack([np.random.permutation(T)[:I] for _ in range(8)])
    idx2 = np.stack([np.random.permutation(T)[:I] for _ in range(8)])
    idx3 = np.stack([np.random.permutation(T)[:I] for _ in range(8)])
    idx4 = np.stack([np.random.permutation(T)[:I] for _ in range(8)])
    fd = mx_kscale(D)
    fk = mx_kscale(K)
    wqp = pack_weight(n((D, K)) * 1.0 / np.sqrt(D) * fd[:, None] * fk, "e4m3")
    keysp = pack_weight(n((K, T)) * 1.0 / np.sqrt(K) / fk[:, None], "e2m1")
    tagsp = pack_weight(n((D, T)) * 0.5 / np.sqrt(D) * fd[:, None], "e4m3")
    return {
        "states": (n((D, Q)) * 0.95 / fd[:, None]).astype(np.float32),
        "wq_words": wqp[0],
        "wq_scales": wqp[1],
        "keys_words": keysp[0],
        "keys_scales": keysp[1],
        "tags_words": tagsp[0],
        "tags_scales": tagsp[1],
        "thr": (np.random.uniform(-0.6, 0.6, (Q, 1))).astype(np.float32),
        "slope": (np.random.uniform(1.0, 3.0, (Q, 1))).astype(np.float32),
        "offs": striped8(idx),
        "offs2": striped8(idx2),
        "offs3": striped8(idx3),
        "offs4": striped8(idx4),
    }


def reference(states, wq_words, wq_scales, keys_words, keys_scales, tags_words, tags_scales, thr, slope, offs, offs2, offs3, offs4):
    idx = unstriped8(offs)
    idx2 = unstriped8(offs2)
    idx3 = unstriped8(offs3)
    idx4 = unstriped8(offs4)
    wqu = unpack_weight(wq_words, wq_scales, "e4m3")
    keysu = unpack_weight(keys_words, keys_scales, "e2m1")
    tagsu = unpack_weight(tags_words, tags_scales, "e4m3")
    statesq = mxq(f64(states), 0, "e4m3")
    qv = wqu.T @ statesq
    qvq = mxq(qv, 0, "e4m3")
    a = qvq.T @ keysu + statesq.T @ tagsu
    f1 = np.zeros((Q, T))
    f1[np.arange(Q)[:, None], idx2[np.arange(Q) % 128 // 16]] = pick8(a, idx, 16)
    cc = a + f1
    s1 = sigmoid(pick8(cc, idx3, 16) * f64(slope) + f64(thr))
    f2 = np.zeros((Q, T))
    f2[np.arange(Q)[:, None], idx[np.arange(Q) % 128 // 16]] = s1
    dd = cc - f2 * 2.0
    y = pick8(dd, idx4, 16)
    return y

@@ -1,0 +1,183 @@
+from contextlib import ExitStack
+
+import concourse.mybir as mybir
+
+D, K, T, SLOTS, Q = 512, 512, 1024, 512, 128
+FLOPS = 2 * D * K * Q + 2 * K * Q * T + 2 * D * Q * T
+
+F32 = mybir.dt.float32
+BF16 = mybir.dt.bfloat16
+I32 = mybir.dt.int32
+U32 = mybir.dt.uint32
+U16 = mybir.dt.uint16
+U8 = mybir.dt.uint8
+FP8X4 = mybir.dt.float8_e4m3fn_x4
+FP4X4 = mybir.dt.float4_e2m1fn_x4
+ALU = mybir.AluOpType
+ACT = mybir.ActivationFunctionType
+
+P = 128
+PACK = 4
+GROUP = 256
+HALF = SLOTS // 2
+HALF_COLS = HALF // 16
+
+
+def load_scale_rows(queues, plane, scales):
+    rows = scales[0].bitcast(I32)
+    for quad in range(4):
+        queues[quad].dma_start(
+            out=plane[:].bitcast(I32)[32 * quad : 32 * quad + 4, :],
+            in_=rows[4 * quad : 4 * quad + 4, :],
+        )
+
+
+def tile_attend_opengate_madeparts_kernel(
+    tc, states, wq_words, wq_scales, keys_words, keys_scales, tags_words, tags_scales,
+    thr, slope, offs, offs2, offs3, offs4, out,
+):
+    nc = tc.nc
+    with ExitStack() as ctx:
+        sb = ctx.enter_context(tc.tile_pool(name="sb", bufs=1))
+        ps = ctx.enter_context(tc.psum_pool(name="ps", bufs=1))
+
+        wq_plane_raw = sb.tile([P, K], U8, align_bytes=64)
+        tags_plane = sb.tile([P, T], U8, align_bytes=64)
+        keys_plane = sb.tile([P, T], U8, align_bytes=64)
+        nc.gpsimd.memset(wq_plane_raw[:].bitcast(U32), 0)
+        nc.gpsimd.memset(tags_plane[:].bitcast(U32), 0)
+        nc.gpsimd.memset(keys_plane[:].bitcast(U32), 0)
+
+        states_raw = sb.tile([P, PACK, Q], F32)
+        nc.sync.dma_start(out=states_raw[:], in_=states.rearrange("(p j) q -> p j q", j=PACK))
+        load_scale_rows([nc.sync] * 4, wq_plane_raw, wq_scales)
+        wq_raw = sb.tile([P, K], I32, align_bytes=64)
+        nc.sync.dma_start(out=wq_raw[:], in_=wq_words[0].rearrange("p n t -> p (n t)").bitcast(I32))
+        tags_codes = sb.tile([P, T], I32, align_bytes=64)
+        nc.sync.dma_start(out=tags_codes[:], in_=tags_words[0].rearrange("p n t -> p (n t)").bitcast(I32))
+        load_scale_rows([nc.sync] * 4, tags_plane, tags_scales)
+        keys_codes = sb.tile([P, 2 * T], U8, align_bytes=64)
+        nc.sync.dma_start(out=keys_codes[:].bitcast(I32), in_=keys_words[0].bitcast(I32))
+        load_scale_rows([nc.sync] * 4, keys_plane, keys_scales)
+
+        list1 = sb.tile([P, SLOTS // 16], U16)
+        list2 = sb.tile([P, SLOTS // 16], U16)
+        list3 = sb.tile([P, SLOTS // 16], U16)
+        list4 = sb.tile([P, SLOTS // 16], U16)
+        nc.sync.dma_start(list1[:], offs)
+        nc.sync.dma_start(list2[:], offs2)
+        nc.sync.dma_start(list3[:], offs3)
+        nc.sync.dma_start(list4[:], offs4)
+        thr_col = sb.tile([P, 1], F32)
+        slope_col = sb.tile([P, 1], F32)
+        nc.sync.dma_start(out=thr_col[:], in_=thr)
+        nc.sync.dma_start(out=slope_col[:], in_=slope)
+
+        f1 = sb.tile([P, T], F32)
+        f2 = sb.tile([P, T], F32)
+        nc.vector.memset(f1[:], 0.0)
+        nc.vector.memset(f2[:], 0.0)
+
+        wq_codes = sb.tile([P, K], U32, align_bytes=64)
+
+        states_bf = sb.tile([P, Q, PACK], BF16, align_bytes=64)
+        nc.vector.tensor_copy(
+            out=states_bf[:].rearrange("p (c i) t -> p c t i", i=4),
+            in_=states_raw[:].rearrange("p t (c i) -> p c t i", i=4),
+        )
+        states_codes = sb.tile([P, Q], U32, align_bytes=64)
+        states_plane = sb.tile([P, Q], U8, align_bytes=64)
+        nc.vector.quantize_mx(
+            out=states_codes[:].bitcast(FP8X4),
+            scales=states_plane[:],
+            in_=states_bf[:].rearrange("p q t -> p (q t)"),
+        )
+
+        wq_plane = sb.tile([P, K], U8, align_bytes=64)
+        nc.vector.tensor_copy(
+            out=wq_plane[:].rearrange("p (t m) -> p t m", t=PACK),
+            in_=wq_plane_raw[:].rearrange("p (m t) -> p t m", t=PACK),
+        )
+        dealt = wq_codes[:].rearrange("p (t c i) -> p c t i", t=PACK, i=4)
+        undealt = wq_raw[:].bitcast(U32).rearrange("p (c i t) -> p c t i", t=PACK, i=4)
+        nc.scalar.copy(out=dealt, in_=undealt)
+
+        qv_bank = ps.tile([P, PACK, Q], F32)
+        for t in range(PACK):
+            cols = slice(t * P, (t + 1) * P)
+            nc.tensor.matmul_mx(
+                out=qv_bank[:, t, :],
+                lhsT=wq_codes[:, cols].bitcast(FP8X4),
+                lhsT_scale=wq_plane[:, cols],
+                rhs=states_codes[:].bitcast(FP8X4),
+                rhs_scale=states_plane[:],
+                start=True,
+                stop=True,
+            )
+        qv_bf = sb.tile([P, Q, PACK], BF16, align_bytes=64)
+        nc.scalar.copy(out=qv_bf[:], in_=qv_bank[:].rearrange("p t q -> p q t"))
+        qv_codes = sb.tile([P, Q], U32, align_bytes=64)
+        qv_plane = sb.tile([P, Q], U8, align_bytes=64)
+        nc.vector.quantize_mx(
+            out=qv_codes[:].bitcast(FP8X4),
+            scales=qv_plane[:],
+            in_=qv_bf[:].rearrange("p q t -> p (q t)"),
+        )
+
+        a_banks = [ps.tile([P, GROUP], F32, name=f"a_bank{b}") for b in range(T // GROUP)]
+        for b, bank in enumerate(a_banks):
+            cols = slice(b * GROUP, (b + 1) * GROUP)
+            nc.tensor.matmul_mx(
+                out=bank[:],
+                lhsT=states_codes[:].bitcast(FP8X4),
+                lhsT_scale=states_plane[:],
+                rhs=tags_codes[:, cols].bitcast(FP8X4),
+                rhs_scale=tags_plane[:, cols],
+                start=True,
+                stop=False,
+            )
+        for b, bank in enumerate(a_banks):
+            cols = slice(b * GROUP, (b + 1) * GROUP)
+            nc.tensor.matmul_mx(
+                out=bank[:],
+                lhsT=qv_codes[:].bitcast(FP8X4),
+                lhsT_scale=qv_plane[:],
+                rhs=keys_codes[:, 2 * b * GROUP : 2 * (b + 1) * GROUP].bitcast(FP4X4),
+                rhs_scale=keys_plane[:, cols],
+                start=False,
+                stop=True,
+            )
+        a = sb.tile([P, T], F32)
+        for b, bank in enumerate(a_banks):
+            cols = slice(b * GROUP, (b + 1) * GROUP)
+            if b % 2 == 0:
+                nc.scalar.copy(out=a[:, cols], in_=bank[:])
+            else:
+                nc.vector.tensor_copy(out=a[:, cols], in_=bank[:])
+
+        halves = [slice(h * HALF_COLS, (h + 1) * HALF_COLS) for h in range(2)]
+        picked = [sb.tile([P, HALF], F32, name=f"picked{h}") for h in range(2)]
+        nc.vector.tensor_copy(picked[0][:], a[:].indirect(list1[:, halves[0]]))
+        nc.scalar.activation(picked[1][:], a[:].indirect(list1[:, halves[1]]), ACT.Copy)
+        for h in range(2):
+            nc.vector.tensor_copy(f1[:].indirect(list2[:, halves[h]]), picked[h][:])
+
+        cc = sb.tile([P, T], F32)
+        nc.vector.tensor_tensor(cc[:], a[:], f1[:], ALU.add)
+
+        gates = [sb.tile([P, HALF], F32, name=f"gates{h}") for h in range(2)]
+        for h in range(2):
+            nc.scalar.activation(
+                gates[h][:], cc[:].indirect(list3[:, halves[h]]), ACT.Sigmoid,
+                bias=thr_col[:], scale=slope_col[:],
+            )
+            nc.vector.tensor_copy(f2[:].indirect(list1[:, halves[h]]), gates[h][:])
+
+        dd = sb.tile([P, T], F32)
+        nc.vector.scalar_tensor_tensor(dd[:], f2[:], -2.0, cc[:], ALU.mult, ALU.add)
+
+        result = [sb.tile([P, HALF], F32, name=f"result{h}") for h in range(2)]
+        nc.vector.tensor_copy(result[0][:], dd[:].indirect(list4[:, halves[0]]))
+        nc.scalar.activation(result[1][:], dd[:].indirect(list4[:, halves[1]]), ACT.Copy)
+        nc.sync.dma_start(out=out[:, 0:HALF], in_=result[0][:])
+        nc.scalar.dma_start(out=out[:, HALF:SLOTS], in_=result[1][:])

@@ -18,15 +18,16 @@ ACT = mybir.ActivationFunctionType
 
 P = 128
 PACK = 4
-GROUP = 256
+GROUP_WIDTHS = (256, 256, 256, 256)
+DEAL_SCALAR = 20
 HALF = SLOTS // 2
 HALF_COLS = HALF // 16
 
 
-def load_scale_rows(queues, plane, scales):
+def load_scale_rows(queue, plane, scales, quads):
     rows = scales[0].bitcast(I32)
-    for quad in range(4):
-        queues[quad].dma_start(
+    for quad in quads:
+        queue.dma_start(
             out=plane[:].bitcast(I32)[32 * quad : 32 * quad + 4, :],
             in_=rows[4 * quad : 4 * quad + 4, :],
         )
@@ -45,20 +46,22 @@ def tile_attend_opengate_madeparts_kernel(
         tags_plane = sb.tile([P, T], U8, align_bytes=64)
         keys_plane = sb.tile([P, T], U8, align_bytes=64)
         nc.gpsimd.memset(wq_plane_raw[:].bitcast(U32), 0)
-        nc.gpsimd.memset(tags_plane[:].bitcast(U32), 0)
         nc.gpsimd.memset(keys_plane[:].bitcast(U32), 0)
+        nc.vector.memset(tags_plane[:].bitcast(U32), 0)
 
         states_raw = sb.tile([P, PACK, Q], F32)
         nc.sync.dma_start(out=states_raw[:], in_=states.rearrange("(p j) q -> p j q", j=PACK))
-        load_scale_rows([nc.sync] * 4, wq_plane_raw, wq_scales)
+        load_scale_rows(nc.sync, wq_plane_raw, wq_scales, range(4))
         wq_raw = sb.tile([P, K], I32, align_bytes=64)
         nc.sync.dma_start(out=wq_raw[:], in_=wq_words[0].rearrange("p n t -> p (n t)").bitcast(I32))
+        load_scale_rows(nc.sync, keys_plane, keys_scales, range(0, 1))
         tags_codes = sb.tile([P, T], I32, align_bytes=64)
         nc.sync.dma_start(out=tags_codes[:], in_=tags_words[0].rearrange("p n t -> p (n t)").bitcast(I32))
-        load_scale_rows([nc.sync] * 4, tags_plane, tags_scales)
+        load_scale_rows(nc.sync, tags_plane, tags_scales, range(4))
         keys_codes = sb.tile([P, 2 * T], U8, align_bytes=64)
         nc.sync.dma_start(out=keys_codes[:].bitcast(I32), in_=keys_words[0].bitcast(I32))
-        load_scale_rows([nc.sync] * 4, keys_plane, keys_scales)
+        load_scale_rows(nc.sync, keys_plane, keys_scales, range(1, 3))
+        load_scale_rows(nc.gpsimd, keys_plane, keys_scales, range(3, 4))
 
         list1 = sb.tile([P, SLOTS // 16], U16)
         list2 = sb.tile([P, SLOTS // 16], U16)
@@ -80,6 +83,11 @@ def tile_attend_opengate_madeparts_kernel(
 
         wq_codes = sb.tile([P, K], U32, align_bytes=64)
 
+        wq_plane = sb.tile([P, K], U8, align_bytes=64)
+        nc.vector.tensor_copy(
+            out=wq_plane[:].rearrange("p (t m) -> p t m", t=PACK),
+            in_=wq_plane_raw[:].rearrange("p (m t) -> p t m", t=PACK),
+        )
         states_bf = sb.tile([P, Q, PACK], BF16, align_bytes=64)
         nc.vector.tensor_copy(
             out=states_bf[:].rearrange("p (c i) t -> p c t i", i=4),
@@ -93,14 +101,10 @@ def tile_attend_opengate_madeparts_kernel(
             in_=states_bf[:].rearrange("p q t -> p (q t)"),
         )
 
-        wq_plane = sb.tile([P, K], U8, align_bytes=64)
-        nc.vector.tensor_copy(
-            out=wq_plane[:].rearrange("p (t m) -> p t m", t=PACK),
-            in_=wq_plane_raw[:].rearrange("p (m t) -> p t m", t=PACK),
-        )
         dealt = wq_codes[:].rearrange("p (t c i) -> p c t i", t=PACK, i=4)
         undealt = wq_raw[:].bitcast(U32).rearrange("p (c i t) -> p c t i", t=PACK, i=4)
-        nc.scalar.copy(out=dealt, in_=undealt)
+        nc.scalar.copy(out=dealt[:, 0:DEAL_SCALAR], in_=undealt[:, 0:DEAL_SCALAR])
+        nc.vector.tensor_copy(out=dealt[:, DEAL_SCALAR:32], in_=undealt[:, DEAL_SCALAR:32])
 
         qv_bank = ps.tile([P, PACK, Q], F32)
         for t in range(PACK):
@@ -124,9 +128,11 @@ def tile_attend_opengate_madeparts_kernel(
             in_=qv_bf[:].rearrange("p q t -> p (q t)"),
         )
 
-        a_banks = [ps.tile([P, GROUP], F32, name=f"a_bank{b}") for b in range(T // GROUP)]
-        for b, bank in enumerate(a_banks):
-            cols = slice(b * GROUP, (b + 1) * GROUP)
+        groups = []
+        for b, width in enumerate(GROUP_WIDTHS):
+            first = sum(GROUP_WIDTHS[:b])
+            groups.append((ps.tile([P, width], F32, name=f"a_bank{b}"), slice(first, first + width)))
+        for b, (bank, cols) in enumerate(groups):
             nc.tensor.matmul_mx(
                 out=bank[:],
                 lhsT=states_codes[:].bitcast(FP8X4),
@@ -136,31 +142,28 @@ def tile_attend_opengate_madeparts_kernel(
                 start=True,
                 stop=False,
             )
-        for b, bank in enumerate(a_banks):
-            cols = slice(b * GROUP, (b + 1) * GROUP)
+        for b, (bank, cols) in enumerate(groups):
             nc.tensor.matmul_mx(
                 out=bank[:],
                 lhsT=qv_codes[:].bitcast(FP8X4),
                 lhsT_scale=qv_plane[:],
-                rhs=keys_codes[:, 2 * b * GROUP : 2 * (b + 1) * GROUP].bitcast(FP4X4),
+                rhs=keys_codes[:, 2 * cols.start : 2 * cols.stop].bitcast(FP4X4),
                 rhs_scale=keys_plane[:, cols],
                 start=False,
                 stop=True,
             )
         a = sb.tile([P, T], F32)
-        for b, bank in enumerate(a_banks):
-            cols = slice(b * GROUP, (b + 1) * GROUP)
-            if b % 2 == 0:
+        for b, (bank, cols) in enumerate(groups):
+            if b in (0, 2):
                 nc.scalar.copy(out=a[:, cols], in_=bank[:])
             else:
                 nc.vector.tensor_copy(out=a[:, cols], in_=bank[:])
 
         halves = [slice(h * HALF_COLS, (h + 1) * HALF_COLS) for h in range(2)]
-        picked = [sb.tile([P, HALF], F32, name=f"picked{h}") for h in range(2)]
-        nc.vector.tensor_copy(picked[0][:], a[:].indirect(list1[:, halves[0]]))
-        nc.scalar.activation(picked[1][:], a[:].indirect(list1[:, halves[1]]), ACT.Copy)
-        for h in range(2):
-            nc.vector.tensor_copy(f1[:].indirect(list2[:, halves[h]]), picked[h][:])
+        picked = sb.tile([P, SLOTS], F32)
+        nc.vector.tensor_copy(picked[:, 0:HALF], a[:].indirect(list1[:, halves[0]]))
+        nc.scalar.activation(picked[:, HALF:SLOTS], a[:].indirect(list1[:, halves[1]]), ACT.Copy)
+        nc.vector.tensor_copy(f1[:].indirect(list2[:]), picked[:])
 
         cc = sb.tile([P, T], F32)
         nc.vector.tensor_tensor(cc[:], a[:], f1[:], ALU.add)

from contextlib import ExitStack

import concourse.mybir as mybir

D, K, T, SLOTS, Q = 512, 512, 1024, 512, 128
FLOPS = 2 * D * K * Q + 2 * K * Q * T + 2 * D * Q * T

F32 = mybir.dt.float32
BF16 = mybir.dt.bfloat16
I32 = mybir.dt.int32
U32 = mybir.dt.uint32
U16 = mybir.dt.uint16
U8 = mybir.dt.uint8
FP8X4 = mybir.dt.float8_e4m3fn_x4
FP4X4 = mybir.dt.float4_e2m1fn_x4
ALU = mybir.AluOpType
ACT = mybir.ActivationFunctionType

P = 128
PACK = 4
GROUP_WIDTHS = (256, 256, 256, 256)
DEAL_SCALAR = 20
HALF = SLOTS // 2
HALF_COLS = HALF // 16


def load_scale_rows(queue, plane, scales, quads):
    rows = scales[0].bitcast(I32)
    for quad in quads:
        queue.dma_start(
            out=plane[:].bitcast(I32)[32 * quad : 32 * quad + 4, :],
            in_=rows[4 * quad : 4 * quad + 4, :],
        )


def tile_attend_opengate_madeparts_kernel(
    tc, states, wq_words, wq_scales, keys_words, keys_scales, tags_words, tags_scales,
    thr, slope, offs, offs2, offs3, offs4, out,
):
    nc = tc.nc
    with ExitStack() as ctx:
        sb = ctx.enter_context(tc.tile_pool(name="sb", bufs=1))
        ps = ctx.enter_context(tc.psum_pool(name="ps", bufs=1))

        wq_plane_raw = sb.tile([P, K], U8, align_bytes=64)
        tags_plane = sb.tile([P, T], U8, align_bytes=64)
        keys_plane = sb.tile([P, T], U8, align_bytes=64)
        nc.gpsimd.memset(wq_plane_raw[:].bitcast(U32), 0)
        nc.gpsimd.memset(keys_plane[:].bitcast(U32), 0)
        nc.vector.memset(tags_plane[:].bitcast(U32), 0)

        states_raw = sb.tile([P, PACK, Q], F32)
        nc.sync.dma_start(out=states_raw[:], in_=states.rearrange("(p j) q -> p j q", j=PACK))
        load_scale_rows(nc.sync, wq_plane_raw, wq_scales, range(4))
        wq_raw = sb.tile([P, K], I32, align_bytes=64)
        nc.sync.dma_start(out=wq_raw[:], in_=wq_words[0].rearrange("p n t -> p (n t)").bitcast(I32))
        load_scale_rows(nc.sync, keys_plane, keys_scales, range(0, 1))
        tags_codes = sb.tile([P, T], I32, align_bytes=64)
        nc.sync.dma_start(out=tags_codes[:], in_=tags_words[0].rearrange("p n t -> p (n t)").bitcast(I32))
        load_scale_rows(nc.sync, tags_plane, tags_scales, range(4))
        keys_codes = sb.tile([P, 2 * T], U8, align_bytes=64)
        nc.sync.dma_start(out=keys_codes[:].bitcast(I32), in_=keys_words[0].bitcast(I32))
        load_scale_rows(nc.sync, keys_plane, keys_scales, range(1, 3))
        load_scale_rows(nc.gpsimd, keys_plane, keys_scales, range(3, 4))

        list1 = sb.tile([P, SLOTS // 16], U16)
        list2 = sb.tile([P, SLOTS // 16], U16)
        list3 = sb.tile([P, SLOTS // 16], U16)
        list4 = sb.tile([P, SLOTS // 16], U16)
        nc.sync.dma_start(list1[:], offs)
        nc.sync.dma_start(list2[:], offs2)
        nc.sync.dma_start(list3[:], offs3)
        nc.sync.dma_start(list4[:], offs4)
        thr_col = sb.tile([P, 1], F32)
        slope_col = sb.tile([P, 1], F32)
        nc.sync.dma_start(out=thr_col[:], in_=thr)
        nc.sync.dma_start(out=slope_col[:], in_=slope)

        f1 = sb.tile([P, T], F32)
        f2 = sb.tile([P, T], F32)
        nc.vector.memset(f1[:], 0.0)
        nc.vector.memset(f2[:], 0.0)

        wq_codes = sb.tile([P, K], U32, align_bytes=64)

        wq_plane = sb.tile([P, K], U8, align_bytes=64)
        nc.vector.tensor_copy(
            out=wq_plane[:].rearrange("p (t m) -> p t m", t=PACK),
            in_=wq_plane_raw[:].rearrange("p (m t) -> p t m", t=PACK),
        )
        states_bf = sb.tile([P, Q, PACK], BF16, align_bytes=64)
        nc.vector.tensor_copy(
            out=states_bf[:].rearrange("p (c i) t -> p c t i", i=4),
            in_=states_raw[:].rearrange("p t (c i) -> p c t i", i=4),
        )
        states_codes = sb.tile([P, Q], U32, align_bytes=64)
        states_plane = sb.tile([P, Q], U8, align_bytes=64)
        nc.vector.quantize_mx(
            out=states_codes[:].bitcast(FP8X4),
            scales=states_plane[:],
            in_=states_bf[:].rearrange("p q t -> p (q t)"),
        )

        dealt = wq_codes[:].rearrange("p (t c i) -> p c t i", t=PACK, i=4)
        undealt = wq_raw[:].bitcast(U32).rearrange("p (c i t) -> p c t i", t=PACK, i=4)
        nc.scalar.copy(out=dealt[:, 0:DEAL_SCALAR], in_=undealt[:, 0:DEAL_SCALAR])
        nc.vector.tensor_copy(out=dealt[:, DEAL_SCALAR:32], in_=undealt[:, DEAL_SCALAR:32])

        qv_bank = ps.tile([P, PACK, Q], F32)
        for t in range(PACK):
            cols = slice(t * P, (t + 1) * P)
            nc.tensor.matmul_mx(
                out=qv_bank[:, t, :],
                lhsT=wq_codes[:, cols].bitcast(FP8X4),
                lhsT_scale=wq_plane[:, cols],
                rhs=states_codes[:].bitcast(FP8X4),
                rhs_scale=states_plane[:],
                start=True,
                stop=True,
            )
        qv_bf = sb.tile([P, Q, PACK], BF16, align_bytes=64)
        nc.scalar.copy(out=qv_bf[:], in_=qv_bank[:].rearrange("p t q -> p q t"))
        qv_codes = sb.tile([P, Q], U32, align_bytes=64)
        qv_plane = sb.tile([P, Q], U8, align_bytes=64)
        nc.vector.quantize_mx(
            out=qv_codes[:].bitcast(FP8X4),
            scales=qv_plane[:],
            in_=qv_bf[:].rearrange("p q t -> p (q t)"),
        )

        groups = []
        for b, width in enumerate(GROUP_WIDTHS):
            first = sum(GROUP_WIDTHS[:b])
            groups.append((ps.tile([P, width], F32, name=f"a_bank{b}"), slice(first, first + width)))
        for b, (bank, cols) in enumerate(groups):
            nc.tensor.matmul_mx(
                out=bank[:],
                lhsT=states_codes[:].bitcast(FP8X4),
                lhsT_scale=states_plane[:],
                rhs=tags_codes[:, cols].bitcast(FP8X4),
                rhs_scale=tags_plane[:, cols],
                start=True,
                stop=False,
            )
        for b, (bank, cols) in enumerate(groups):
            nc.tensor.matmul_mx(
                out=bank[:],
                lhsT=qv_codes[:].bitcast(FP8X4),
                lhsT_scale=qv_plane[:],
                rhs=keys_codes[:, 2 * cols.start : 2 * cols.stop].bitcast(FP4X4),
                rhs_scale=keys_plane[:, cols],
                start=False,
                stop=True,
            )
        a = sb.tile([P, T], F32)
        for b, (bank, cols) in enumerate(groups):
            if b in (0, 2):
                nc.scalar.copy(out=a[:, cols], in_=bank[:])
            else:
                nc.vector.tensor_copy(out=a[:, cols], in_=bank[:])

        halves = [slice(h * HALF_COLS, (h + 1) * HALF_COLS) for h in range(2)]
        picked = sb.tile([P, SLOTS], F32)
        nc.vector.tensor_copy(picked[:, 0:HALF], a[:].indirect(list1[:, halves[0]]))
        nc.scalar.activation(picked[:, HALF:SLOTS], a[:].indirect(list1[:, halves[1]]), ACT.Copy)
        nc.vector.tensor_copy(f1[:].indirect(list2[:]), picked[:])

        cc = sb.tile([P, T], F32)
        nc.vector.tensor_tensor(cc[:], a[:], f1[:], ALU.add)

        gates = [sb.tile([P, HALF], F32, name=f"gates{h}") for h in range(2)]
        for h in range(2):
            nc.scalar.activation(
                gates[h][:], cc[:].indirect(list3[:, halves[h]]), ACT.Sigmoid,
                bias=thr_col[:], scale=slope_col[:],
            )
            nc.vector.tensor_copy(f2[:].indirect(list1[:, halves[h]]), gates[h][:])

        dd = sb.tile([P, T], F32)
        nc.vector.scalar_tensor_tensor(dd[:], f2[:], -2.0, cc[:], ALU.mult, ALU.add)

        result = [sb.tile([P, HALF], F32, name=f"result{h}") for h in range(2)]
        nc.vector.tensor_copy(result[0][:], dd[:].indirect(list4[:, halves[0]]))
        nc.scalar.activation(result[1][:], dd[:].indirect(list4[:, halves[1]]), ACT.Copy)
        nc.sync.dma_start(out=out[:, 0:HALF], in_=result[0][:])
        nc.scalar.dma_start(out=out[:, HALF:SLOTS], in_=result[1][:])
